import numpy as np
import ml_dtypes


def mxq(x, axis, fmt="e4m3"):
    dtype, down = {"e4m3": (ml_dtypes.float8_e4m3fn, 7), "e5m2": (ml_dtypes.float8_e5m2, 14)}[fmt]
    v = np.moveaxis(np.asarray(x, np.float32).astype(ml_dtypes.bfloat16).astype(np.float64), axis, -1)
    blocks = v.reshape(v.shape[:-1] + (-1, 32))
    amax = np.abs(blocks).max(-1, keepdims=True)
    byte = np.maximum(np.where(amax > 0, np.frexp(amax)[1] - 1 + 127, 0) - down, 1)
    scale = np.exp2(byte - 127.0)
    codes = (blocks / scale).astype(np.float32).astype(dtype).astype(np.float64)
    return np.moveaxis((codes * scale).reshape(v.shape), -1, axis)


WIDE = False


def mx_kscale(k):
    if not WIDE:
        return np.ones(k)
    levels = np.array([10, -10, 5, -5, 0])
    if k % 512:
        return np.exp2(np.random.permutation(np.resize(levels, k // 32))).repeat(32)
    a = np.empty((k // 512, 16))
    for p in range(k // 512):
        a[p, :8] = np.random.permutation(np.resize(levels, 8))
        for g in range(8):
            far = levels[np.abs(levels - a[p, g]) >= 10]
            a[p, g + 8] = far[np.random.randint(len(far))]
    return np.exp2(a.ravel()).repeat(32)


def f64(x):
    return np.asarray(x).astype(np.float64)


def striped(idx):
    return np.tile(idx.reshape(-1, 16).T, (8, 1)).astype(np.uint16)


def unstriped(offs):
    return offs[:16].T.reshape(-1).astype(np.int64)


E2M1 = np.array([0.0, 0.5, 1.0, 1.5, 2.0, 3.0, 4.0, 6.0, -0.0, -0.5, -1.0, -1.5, -2.0, -3.0, -4.0, -6.0])


def pack_weight(w, fmt):
    k, n = w.shape
    w = f64(np.asarray(w, np.float32).astype(ml_dtypes.bfloat16)).reshape(k // 32, 32, n)
    amax = np.abs(w).max(1)
    if fmt == "e4m3":
        byte = np.frexp(amax)[1] - 1 + 127 - 7
    else:
        mant, ex = np.frexp(amax / 6.0)
        byte = np.where(mant > 0.5, ex, ex - 1) + 127
    byte = np.clip(np.where(amax > 0, byte, 1), 1, 254)
    scaled = (w * np.exp2(127.0 - byte)[:, None, :]).reshape(k, n).astype(np.float32)
    by_word = np.ascontiguousarray(scaled.reshape(k // 512, 128, 4, n).transpose(0, 1, 3, 2))
    if fmt == "e4m3":
        words = by_word.astype(ml_dtypes.float8_e4m3fn).view(np.uint8)
    else:
        c = by_word.astype(ml_dtypes.float4_e2m1fn).view(np.uint8) & 0xF
        words = (c[..., 0::2] | (c[..., 1::2] << 4)).reshape(k // 512, 128, 2 * n)
    return np.ascontiguousarray(words), np.ascontiguousarray(byte.astype(np.uint8).reshape(k // 512, 16, n))


def unpack_weight(words, scales, fmt):
    g, _, n = scales.shape
    words = np.ascontiguousarray(words).reshape(g, 128, n, -1)
    if fmt == "e4m3":
        vals = words.view(ml_dtypes.float8_e4m3fn).astype(np.float64)
    else:
        nib = np.empty((g, 128, n, 4), np.uint8)
        nib[..., 0::2] = words & 0xF
        nib[..., 1::2] = words >> 4
        vals = E2M1[nib]
    vals = vals * np.repeat(np.exp2(scales.astype(np.float64) - 127.0), 8, axis=1)[..., None]
    return vals.transpose(0, 1, 3, 2).reshape(g * 512, n)


def gelu(v):
    return 0.5 * v * (1.0 + np.tanh(np.sqrt(2.0 / np.pi) * (v + 0.044715 * v**3)))


K, H, N, T, S = 512, 1024, 512, 2048, 1024

def setup_inputs():
    n = np.random.standard_normal
    s = mx_kscale(K)[:, None]
    u = mx_kscale(H)[:, None]
    tab_words, tab_scales = pack_weight(n((K, T)) * s, "e4m3")
    w2_words, w2_scales = pack_weight(n((K, H)) / s / K ** 0.5, "e2m1")
    w3_words, w3_scales = pack_weight(n((K, H)) * u.T / s / K ** 0.5, "e4m3")
    return {
        "tab_words": tab_words, "tab_scales": tab_scales,
        "offs": striped(np.random.permutation(T)[:S]),
        "offs2": striped(np.random.permutation(T)[:S]),
        "offs3": striped(np.random.permutation(T)[:S]),
        "w1": (n((K, H)) / s / K ** 0.5).astype(np.float32),
        "w2_words": w2_words, "w2_scales": w2_scales,
        "w3_words": w3_words, "w3_scales": w3_scales,
        "g": (np.exp(0.3 * n(H)) * u[:, 0]).astype(np.float32),
        "w4": (n((H, N)) / u / H ** 0.5).astype(np.float32),
    }

def reference(tab_words, tab_scales, offs, offs2, offs3, w1, w2_words, w2_scales, w3_words, w3_scales, g, w4):
    vc = unpack_weight(tab_words, tab_scales, "e4m3")[:, unstriped(offs)]
    vl = unpack_weight(tab_words, tab_scales, "e4m3")[:, unstriped(offs2)]
    vr = unpack_weight(tab_words, tab_scales, "e4m3")[:, unstriped(offs3)]
    a = mxq(f64(w1), 0, "e4m3").T @ vc
    b = unpack_weight(w2_words, w2_scales, "e2m1").T @ vl
    c = unpack_weight(w3_words, w3_scales, "e4m3").T @ vr
    a2, b2 = np.square([a, b])
    h = f64(g)[:, None] * np.log1p(a2 + b2) + c
    return mxq(f64(w4), 0, "e4m3").T @ mxq(h, 0, "e4m3")

@@ -1,0 +1,322 @@
+from contextlib import ExitStack
+
+import concourse.mybir as mybir
+from concourse.masks import make_identity
+
+K, H, N, T, S = 512, 1024, 512, 2048, 1024
+FLOPS = 2 * K * H * S * 3 + 2 * H * N * S
+
+F32 = mybir.dt.float32
+BF16 = mybir.dt.bfloat16
+I32 = mybir.dt.int32
+U32 = mybir.dt.uint32
+U16 = mybir.dt.uint16
+U8 = mybir.dt.uint8
+FP8X4 = mybir.dt.float8_e4m3fn_x4
+FP4X4 = mybir.dt.float4_e2m1fn_x4
+ACT = mybir.ActivationFunctionType
+ALU = mybir.AluOpType
+
+P = 128
+PACK = 4
+PASS = P * PACK
+BANK = 512
+HALVES = H // PASS
+GROUPS = [256,512,256]
+
+
+def tile_list_codebook_phoneme_logits_kernel(
+    tc, tab_words, tab_scales, offs, offs2, offs3, w1, w2_words, w2_scales, w3_words, w3_scales, g, w4, out
+):
+    nc = tc.nc
+    with ExitStack() as ctx:
+        keep = ctx.enter_context(tc.tile_pool(name="keep", bufs=1))
+        work = ctx.enter_context(tc.tile_pool(name="work", bufs=1))
+        psum = ctx.enter_context(tc.psum_pool(name="psum", bufs=1))
+
+        cur_list = keep.tile([P, S // 16], U16, name="cur_list")
+        left_list = keep.tile([P, S // 16], U16, name="left_list")
+        right_list = keep.tile([P, S // 16], U16, name="right_list")
+        tab_w = keep.tile([P, T], I32, name="tab_w", align_bytes=64)
+        tab_s = keep.tile([P, T], U8, name="tab_s", align_bytes=64)
+        w2_w = keep.tile([P, 2 * H], U8, name="w2_w", align_bytes=64)
+        w2_s = keep.tile([P, H], U8, name="w2_s", align_bytes=64)
+        w3_w_raw = keep.tile([P, H], I32, name="w3_w_raw", align_bytes=64)
+        w3_s_raw = keep.tile([P, H], U8, name="w3_s_raw", align_bytes=64)
+        w3_w = keep.tile([P, H], I32, name="w3_w", align_bytes=64)
+        w3_s = keep.tile([P, H], U8, name="w3_s", align_bytes=64)
+        gain = keep.tile([P, HALVES, PACK], F32, name="gain")
+        ident = keep.tile([P, P], F32, name="ident", align_bytes=64)
+        one = keep.tile([P, 1], F32, name="one")
+        warm = keep.tile([P, 1], F32, name="warm")
+        w1_raw = [keep.tile([P, PACK, PASS], F32, name=f"w1_raw{b}", align_bytes=64) for b in range(HALVES)]
+        w4_raw = [keep.tile([P, PACK, N], F32, name=f"w4_raw{b}", align_bytes=64) for b in range(HALVES)]
+        w1_q = [keep.tile([P, PASS], U32, name=f"w1_q{b}", align_bytes=64) for b in range(HALVES)]
+        w1_s = [keep.tile([P, PASS], U8, name=f"w1_s{b}", align_bytes=64) for b in range(HALVES)]
+        w4_q = [keep.tile([P, N], U32, name=f"w4_q{b}", align_bytes=64) for b in range(HALVES)]
+        w4_s = [keep.tile([P, N], U8, name=f"w4_s{b}", align_bytes=64) for b in range(HALVES)]
+
+        def load_scales(queue, plane, rows):
+            for q in range(4):
+                queue.dma_start(plane[32 * q : 32 * q + 4, :].bitcast(I32), rows[0, 4 * q : 4 * q + 4, :].bitcast(I32))
+
+        def interleave(engine, dst, src):
+            o = dst.rearrange("p (c i) t -> p c t i", i=4)
+            i_ = src.rearrange("p t (c i) -> p c t i", i=4)
+            if engine == "v":
+                nc.vector.tensor_copy(o, i_)
+            elif engine == "s":
+                nc.scalar.activation(o, i_, ACT.Copy)
+            else:
+                nc.gpsimd.tensor_scalar(o, i_, 1.0, 0.0, ALU.mult, ALU.add)
+
+        def quantize(codes, scales, grouped):
+            nc.vector.quantize_mx(codes.bitcast(FP8X4), scales, grouped.rearrange("p c t -> p (c t)"))
+
+        nc.vector.memset(tab_s[:].bitcast(I32), 0)
+        nc.vector.memset(one[:], 1.0)
+        nc.vector.memset(w2_s[:].bitcast(I32), 0)
+        nc.vector.memset(w3_s_raw[:].bitcast(I32), 0)
+        load_scales(nc.scalar, tab_s, tab_scales)
+        nc.scalar.activation(warm[:], one[:], ACT.Ln)
+        make_identity(nc, ident[:])
+        w1_rows = w1.rearrange("(p j) c -> p j c", j=PACK)
+        nc.sync.dma_start(cur_list[:], offs)
+        nc.sync.dma_start(left_list[:], offs2)
+        nc.sync.dma_start(w1_raw[0][:], w1_rows[:, :, 0:PASS])
+        nc.sync.dma_start(tab_w[:], tab_words[0].rearrange("p t i -> p (t i)").bitcast(I32))
+        nc.sync.dma_start(w2_w[:].bitcast(I32), w2_words[0].bitcast(I32))
+        load_scales(nc.sync, w2_s, w2_scales)
+        nc.sync.dma_start(right_list[:], offs3)
+        nc.sync.dma_start(w3_w_raw[:], w3_words[0].rearrange("p e i -> p (e i)").bitcast(I32))
+        nc.sync.dma_start(w1_raw[1][:], w1_rows[:, :, PASS:H])
+        load_scales(nc.sync, w3_s_raw, w3_scales)
+        nc.sync.dma_start(gain[:], g.rearrange("(b p t) -> p b t", b=HALVES, t=PACK))
+        for b in range(HALVES):
+            nc.sync.dma_start(w4_raw[b][:], w4[b * PASS : (b + 1) * PASS, :].rearrange("(p j) n -> p j n", j=PACK))
+
+        banks = [psum.tile([P, BANK], F32, name=f"bank{i}") for i in range(8)]
+        rings = {"ab": banks[0:4], "energy": banks[4:6], "c": banks[6:8]}
+        turns = {name: 0 for name in rings}
+
+        def next_bank(name):
+            ring = rings[name]
+            turns[name] += 1
+            return ring[(turns[name] - 1) % len(ring)]
+
+        starts = [sum(GROUPS[:i]) for i in range(len(GROUPS))]
+        picked = {}
+
+        def gather_scales(name, lst, gi):
+            n, j0 = GROUPS[gi], starts[gi]
+            tile = keep.tile([P, n], U8, name=f"{name}_s{gi}", align_bytes=64)
+            nc.vector.tensor_copy(tile[:], tab_s[:].indirect(lst[:, j0 // 16 : (j0 + n) // 16]))
+            picked[(name, "s", gi)] = tile
+
+        def gather_words(name, lst, gi):
+            n, j0 = GROUPS[gi], starts[gi]
+            tile = keep.tile([P, n], U32, name=f"{name}_w{gi}", align_bytes=64)
+            nc.vector.tensor_copy(tile[:], tab_w[:].bitcast(U32).indirect(lst[:, j0 // 16 : (j0 + n) // 16]))
+            picked[(name, "w", gi)] = tile
+
+        lists = {"left": left_list, "cur": cur_list, "right": right_list}
+
+        def gather(name, gi):
+            gather_scales(name, lists[name], gi)
+            gather_words(name, lists[name], gi)
+
+        grouped = {}
+
+        def cast_weight(name, raw, engine):
+            tile = keep.tile([P, raw.shape[2], PACK], BF16, name=f"{name}_bf", align_bytes=64)
+            interleave(engine, tile[:], raw[:])
+            grouped[name] = tile
+
+        squares = {}
+
+        def square(which, gi, b, jt):
+            bank = next_bank("ab")
+            cols = slice(jt * P, (jt + 1) * P)
+            if which == "cur":
+                rhs, rhs_scale = w1_q[b][:].bitcast(FP8X4), w1_s[b][:]
+            else:
+                rhs = w2_w[:, 2 * b * PASS : 2 * (b + 1) * PASS].bitcast(FP4X4)
+                rhs_scale = w2_s[:, b * PASS : (b + 1) * PASS]
+            nc.tensor.matmul_mx(
+                bank[:],
+                lhsT=picked[(which, "w", gi)][:, cols].bitcast(FP8X4),
+                lhsT_scale=picked[(which, "s", gi)][:, cols],
+                rhs=rhs,
+                rhs_scale=rhs_scale,
+                start=True,
+                stop=True,
+            )
+            sq = work.tile([P, PACK, P], F32, name="sq", tag="sq", bufs=32, align_bytes=64)
+            nc.scalar.activation(sq[:], bank[:].rearrange("p (m t) -> p t m", t=PACK), ACT.Square)
+            squares[(which, gi, b, jt)] = sq
+
+        planes = {}
+
+        logged = {}
+
+        def energy_log(gi, b, step):
+            n = GROUPS[gi]
+            per_bank = BANK // n
+            ts = range(step * per_bank, (step + 1) * per_bank)
+            energy = next_bank("energy")[:].rearrange("p (i n) -> p i n", n=n)
+            for i, t in enumerate(ts):
+                for jt in reversed(range(n // P)):
+                    for which in ("cur", "left"):
+                        nc.tensor.matmul(
+                            energy[:, i, jt * P : (jt + 1) * P],
+                            lhsT=squares[(which, gi, b, jt)][:, t, :],
+                            rhs=ident[:],
+                            start=(which == "cur"),
+                            stop=(which == "left"),
+                            is_transpose=True,
+                        )
+            logs = work.tile([P, per_bank, n], F32, name="logs", tag="logs", bufs=4, align_bytes=64)
+            nc.scalar.activation(logs[:], energy, ACT.Ln, bias=one[:])
+            logged[(gi, b, step)] = logs
+
+        def finish(gi, b, step):
+            n = GROUPS[gi]
+            per_bank = BANK // n
+            ts = range(step * per_bank, (step + 1) * per_bank)
+            logs = logged[(gi, b, step)]
+            c_bank = next_bank("c")[:].rearrange("p (i n) -> p i n", n=n)
+            for i, t in enumerate(ts):
+                cols = slice(b * PASS + t * P, b * PASS + (t + 1) * P)
+                nc.tensor.matmul_mx(
+                    c_bank[:, i, :],
+                    lhsT=w3_w[:, cols].bitcast(FP8X4),
+                    lhsT_scale=w3_s[:, cols],
+                    rhs=picked[("right", "w", gi)][:].bitcast(FP8X4),
+                    rhs_scale=picked[("right", "s", gi)][:],
+                    start=True,
+                    stop=True,
+                )
+            if step == 0:
+                planes[(gi, b)] = work.tile([P, PACK, n], BF16, name="h_planes", tag="h_planes", bufs=3, align_bytes=64)
+            for i, t in enumerate(ts):
+                nc.vector.scalar_tensor_tensor(
+                    planes[(gi, b)][:, t, :], logs[:, i, :], gain[:, b, t : t + 1], c_bank[:, i, :], ALU.mult, ALU.add
+                )
+
+        def hidden_pair(gi, b, step):
+            energy_log(gi, b, step)
+            energy_log(gi, b, step + 1)
+            finish(gi, b, step)
+            finish(gi, b, step + 1)
+
+        def squares_of(gi, b, jts):
+            for jt in jts:
+                square("left", gi, b, jt)
+                square("cur", gi, b, jt)
+
+        h_grouped = {}
+        h_q = {}
+
+        def group_hidden(gi, b, engine):
+            tile = work.tile([P, GROUPS[gi], PACK], BF16, name="h_grouped", tag="h_grouped", bufs=2, align_bytes=64)
+            interleave(engine, tile[:], planes[(gi, b)][:])
+            h_grouped[(gi, b)] = tile
+
+        def quantize_hidden(gi, b):
+            codes = work.tile([P, GROUPS[gi]], U32, name="h_codes", tag="h_codes", bufs=4, align_bytes=64)
+            scales = work.tile([P, GROUPS[gi]], U8, name="h_scales", tag="h_scales", bufs=4, align_bytes=64)
+            quantize(codes[:], scales[:], h_grouped[(gi, b)][:])
+            h_q[(gi, b)] = (codes, scales)
+
+        def classify(gi, step, engine, ring="ab"):
+            n, j0 = GROUPS[gi], starts[gi]
+            per_bank = BANK // n
+            bank = next_bank(ring)[:].rearrange("p (i n) -> p i n", n=n)
+            for i in range(per_bank):
+                cols = slice((step * per_bank + i) * P, (step * per_bank + i + 1) * P)
+                for b in range(HALVES):
+                    codes, scales = h_q[(gi, b)]
+                    nc.tensor.matmul_mx(
+                        bank[:, i, :],
+                        lhsT=w4_q[b][:, cols].bitcast(FP8X4),
+                        lhsT_scale=w4_s[b][:, cols],
+                        rhs=codes[:].bitcast(FP8X4),
+                        rhs_scale=scales[:],
+                        start=(b == 0),
+                        stop=(b == HALVES - 1),
+                    )
+            logits = work.tile([P, per_bank, n], F32, name="logits", tag="logits", bufs=4, align_bytes=64)
+            if engine == "v":
+                nc.vector.tensor_copy(logits[:], bank)
+            else:
+                nc.scalar.copy(logits[:], bank)
+            rows = out[step * per_bank * P : (step + 1) * per_bank * P, j0 : j0 + n]
+            nc.sync.dma_start(rows.rearrange("(i p) j -> p i j", p=P), logits[:])
+
+        def permute_w3():
+            nc.vector.tensor_copy(
+                w3_w[:].rearrange("p (b t m) -> p b t m", b=HALVES, t=PACK),
+                w3_w_raw[:].rearrange("p (b m t) -> p b t m", b=HALVES, t=PACK),
+            )
+            nc.vector.tensor_copy(
+                w3_s[:].rearrange("p (b t m) -> p b t m", b=HALVES, t=PACK),
+                w3_s_raw[:].rearrange("p (b m t) -> p b t m", b=HALVES, t=PACK),
+            )
+
+        gather_scales("cur", cur_list, 0)
+        gather_scales("left", left_list, 0)
+        cast_weight("w1_0", w1_raw[0], "s")
+        quantize(w1_q[0][:], w1_s[0][:], grouped["w1_0"][:])
+        gather_words("cur", cur_list, 0)
+        gather_words("left", left_list, 0)
+        for jt in range(2):
+            square("cur", 0, 0, jt)
+        for jt in range(2):
+            square("left", 0, 0, jt)
+        gather("cur", 1)
+        gather("left", 1)
+        gather("right", 0)
+        cast_weight("w1_1", w1_raw[1], "v")
+        permute_w3()
+        quantize(w1_q[1][:], w1_s[1][:], grouped["w1_1"][:])
+        squares_of(1, 0, (0, 1))
+        hidden_pair(0, 0, 0)
+        squares_of(1, 0, (2, 3))
+        gather("right", 1)
+        group_hidden(0, 0, "v")
+        hidden_pair(1, 0, 0)
+        quantize_hidden(0, 0)
+        squares_of(0, 1, (0, 1))
+        gather("cur", 2)
+        hidden_pair(1, 0, 2)
+        squares_of(1, 1, (0, 1))
+        cast_weight("w4_0", w4_raw[0], "s")
+        gather("left", 2)
+        group_hidden(1, 0, "v")
+        hidden_pair(0, 1, 0)
+        squares_of(1, 1, (2, 3))
+        quantize_hidden(1, 0)
+        quantize(w4_q[0][:], w4_s[0][:], grouped["w4_0"][:])
+        cast_weight("w4_1", w4_raw[1], "v")
+        group_hidden(0, 1, "v")
+        gather("right", 2)
+        hidden_pair(1, 1, 0)
+        squares_of(2, 0, (0, 1))
+        quantize_hidden(0, 1)
+        quantize(w4_q[1][:], w4_s[1][:], grouped["w4_1"][:])
+        hidden_pair(1, 1, 2)
+        squares_of(2, 1, (0, 1))
+        group_hidden(1, 1, "v")
+        hidden_pair(2, 0, 0)
+        classify(0, 0, "ss"[0])
+        classify(0, 1, "ss"[1])
+        quantize_hidden(1, 1)
+        group_hidden(2, 0, "v")
+        hidden_pair(2, 1, 0)
+        quantize_hidden(2, 0)
+        group_hidden(2, 1, "v")
+        quantize_hidden(2, 1)
+        for step in range(4):
+            classify(1, step, "ssss"[step])
+        classify(2, 0, "v", "c")
+        classify(2, 1, "s", "c")

@@ -22,7 +22,7 @@ PACK = 4
 PASS = P * PACK
 BANK = 512
 HALVES = H // PASS
-GROUPS = [256,512,256]
+GROUPS = [256, 512, 256]
 
 
 def tile_list_codebook_phoneme_logits_kernel(
@@ -73,27 +73,28 @@ def tile_list_codebook_phoneme_logits_kernel(
         def quantize(codes, scales, grouped):
             nc.vector.quantize_mx(codes.bitcast(FP8X4), scales, grouped.rearrange("p c t -> p (c t)"))
 
-        nc.vector.memset(tab_s[:].bitcast(I32), 0)
+        nc.gpsimd.memset(tab_s[:].bitcast(I32), 0)
         nc.vector.memset(one[:], 1.0)
         nc.vector.memset(w2_s[:].bitcast(I32), 0)
         nc.vector.memset(w3_s_raw[:].bitcast(I32), 0)
-        load_scales(nc.scalar, tab_s, tab_scales)
         nc.scalar.activation(warm[:], one[:], ACT.Ln)
         make_identity(nc, ident[:])
         w1_rows = w1.rearrange("(p j) c -> p j c", j=PACK)
-        nc.sync.dma_start(cur_list[:], offs)
+        w4_rows = w4.rearrange("(b p j) n -> b p j n", b=HALVES, j=PACK)
         nc.sync.dma_start(left_list[:], offs2)
-        nc.sync.dma_start(w1_raw[0][:], w1_rows[:, :, 0:PASS])
-        nc.sync.dma_start(tab_w[:], tab_words[0].rearrange("p t i -> p (t i)").bitcast(I32))
         nc.sync.dma_start(w2_w[:].bitcast(I32), w2_words[0].bitcast(I32))
+        load_scales(nc.sync, tab_s, tab_scales)
+        nc.sync.dma_start(tab_w[:], tab_words[0].rearrange("p t i -> p (t i)").bitcast(I32))
         load_scales(nc.sync, w2_s, w2_scales)
+        nc.sync.dma_start(w1_raw[0][:], w1_rows[:, :, 0:PASS])
+        nc.sync.dma_start(cur_list[:], offs)
+        nc.sync.dma_start(w1_raw[1][:], w1_rows[:, :, PASS:H])
         nc.sync.dma_start(right_list[:], offs3)
         nc.sync.dma_start(w3_w_raw[:], w3_words[0].rearrange("p e i -> p (e i)").bitcast(I32))
-        nc.sync.dma_start(w1_raw[1][:], w1_rows[:, :, PASS:H])
+        nc.sync.dma_start(w4_raw[0][:], w4_rows[0])
+        nc.sync.dma_start(w4_raw[1][:], w4_rows[1])
         load_scales(nc.sync, w3_s_raw, w3_scales)
         nc.sync.dma_start(gain[:], g.rearrange("(b p t) -> p b t", b=HALVES, t=PACK))
-        for b in range(HALVES):
-            nc.sync.dma_start(w4_raw[b][:], w4[b * PASS : (b + 1) * PASS, :].rearrange("(p j) n -> p j n", j=PACK))
 
         banks = [psum.tile([P, BANK], F32, name=f"bank{i}") for i in range(8)]
         rings = {"ab": banks[0:4], "energy": banks[4:6], "c": banks[6:8]}
@@ -127,10 +128,11 @@ def tile_list_codebook_phoneme_logits_kernel(
 
         grouped = {}
 
-        def cast_weight(name, raw, engine):
-            tile = keep.tile([P, raw.shape[2], PACK], BF16, name=f"{name}_bf", align_bytes=64)
-            interleave(engine, tile[:], raw[:])
-            grouped[name] = tile
+        def cast_weight(name, raw, engine, part=0, parts=1):
+            if name not in grouped:
+                grouped[name] = keep.tile([P, PASS, PACK], BF16, name=f"{name}_bf", align_bytes=64)
+            cols = slice(part * PASS // parts, (part + 1) * PASS // parts)
+            interleave(engine, grouped[name][:, cols, :], raw[:, :, cols])
 
         squares = {}
 
@@ -151,9 +153,73 @@ def tile_list_codebook_phoneme_logits_kernel(
                 start=True,
                 stop=True,
             )
-            sq = work.tile([P, PACK, P], F32, name="sq", tag="sq", bufs=32, align_bytes=64)
+            sq = work.tile([P, PACK, P], F32, name="sq", tag="sq", bufs=26, align_bytes=64)
             nc.scalar.activation(sq[:], bank[:].rearrange("p (m t) -> p t m", t=PACK), ACT.Square)
             squares[(which, gi, b, jt)] = sq
+
+        w2p_w = [keep.tile([P, 2 * PASS], U8, name=f"w2p_w{b}", align_bytes=64) for b in range(HALVES)]
+        w2p_s = [keep.tile([P, PASS], U8, name=f"w2p_s{b}", align_bytes=64) for b in range(HALVES)]
+
+        def permute_w2(b):
+            nc.vector.tensor_copy(
+                w2p_w[b][:].rearrange("p (t m e) -> p t m e", t=PACK, e=2),
+                w2_w[:, 2 * b * PASS : 2 * (b + 1) * PASS].rearrange("p (m t e) -> p t m e", t=PACK, e=2),
+            )
+            nc.vector.tensor_copy(
+                w2p_s[b][:].rearrange("p (t m) -> p t m", t=PACK),
+                w2_s[:, b * PASS : (b + 1) * PASS].rearrange("p (m t) -> p t m", t=PACK),
+            )
+
+        def cast_permuted(name, raw, engine):
+            tile = keep.tile([P, PASS, PACK], BF16, name=f"{name}_bf", align_bytes=64)
+            o = tile[:].rearrange("p (t m) j -> p m j t", t=PACK)
+            i_ = raw[:].rearrange("p j (m t) -> p m j t", t=PACK)
+            if engine == "v":
+                nc.vector.tensor_copy(o, i_)
+            elif engine == "s":
+                nc.scalar.activation(o, i_, ACT.Copy)
+            else:
+                nc.gpsimd.tensor_scalar(o, i_, 1.0, 0.0, ALU.mult, ALU.add)
+            grouped[name] = tile
+
+        direct = {}
+
+        def square_direct(which, gi, b, step):
+            n = GROUPS[gi]
+            per_bank = BANK // n
+            bank = next_bank("ab")[:]
+            for i in range(per_bank):
+                t = step * per_bank + i
+                if which == "cur":
+                    lhsT, lhsT_scale = w1_q[b][:, t * P : (t + 1) * P].bitcast(FP8X4), w1_s[b][:, t * P : (t + 1) * P]
+                else:
+                    lhsT, lhsT_scale = w2p_w[b][:, 2 * t * P : 2 * (t + 1) * P].bitcast(FP4X4), w2p_s[b][:, t * P : (t + 1) * P]
+                nc.tensor.matmul_mx(
+                    bank[:, i * n : (i + 1) * n],
+                    lhsT=lhsT,
+                    lhsT_scale=lhsT_scale,
+                    rhs=picked[(which, "w", gi)][:].bitcast(FP8X4),
+                    rhs_scale=picked[(which, "s", gi)][:],
+                    start=True,
+                    stop=True,
+                )
+            sq = work.tile([P, BANK], F32, name="sqd", tag="sqd", bufs=8, align_bytes=64)
+            nc.scalar.activation(sq[:], bank, ACT.Square)
+            direct[(which, gi, b, step)] = sq
+
+        summed = {}
+
+        def add_direct(gi, b, step, engine):
+            total = work.tile([P, BANK], F32, name="total", tag="total", bufs=4, align_bytes=64)
+            eng = nc.vector if engine == "v" else nc.gpsimd
+            eng.tensor_tensor(total[:], direct[("cur", gi, b, step)][:], direct[("left", gi, b, step)][:], ALU.add)
+            summed[(gi, b, step)] = total
+
+        def log_direct(gi, b, step):
+            n = GROUPS[gi]
+            logs = work.tile([P, BANK // n, n], F32, name="logs", tag="logs", bufs=10, align_bytes=64)
+            nc.scalar.activation(logs[:].rearrange("p i n -> p (i n)"), summed[(gi, b, step)][:], ACT.Ln, bias=one[:])
+            logged[(gi, b, step)] = logs
 
         planes = {}
 
@@ -175,16 +241,16 @@ def tile_list_codebook_phoneme_logits_kernel(
                             stop=(which == "left"),
                             is_transpose=True,
                         )
-            logs = work.tile([P, per_bank, n], F32, name="logs", tag="logs", bufs=4, align_bytes=64)
+            logs = work.tile([P, per_bank, n], F32, name="logs", tag="logs", bufs=10, align_bytes=64)
             nc.scalar.activation(logs[:], energy, ACT.Ln, bias=one[:])
             logged[(gi, b, step)] = logs
 
-        def finish(gi, b, step):
+        def finish(gi, b, step, ring="c"):
             n = GROUPS[gi]
             per_bank = BANK // n
             ts = range(step * per_bank, (step + 1) * per_bank)
             logs = logged[(gi, b, step)]
-            c_bank = next_bank("c")[:].rearrange("p (i n) -> p i n", n=n)
+            c_bank = next_bank(ring)[:].rearrange("p (i n) -> p i n", n=n)
             for i, t in enumerate(ts):
                 cols = slice(b * PASS + t * P, b * PASS + (t + 1) * P)
                 nc.tensor.matmul_mx(
@@ -218,13 +284,13 @@ def tile_list_codebook_phoneme_logits_kernel(
         h_q = {}
 
         def group_hidden(gi, b, engine):
-            tile = work.tile([P, GROUPS[gi], PACK], BF16, name="h_grouped", tag="h_grouped", bufs=2, align_bytes=64)
+            tile = work.tile([P, GROUPS[gi], PACK], BF16, name="h_grouped", tag="h_grouped", bufs=3, align_bytes=64)
             interleave(engine, tile[:], planes[(gi, b)][:])
             h_grouped[(gi, b)] = tile
 
         def quantize_hidden(gi, b):
-            codes = work.tile([P, GROUPS[gi]], U32, name="h_codes", tag="h_codes", bufs=4, align_bytes=64)
-            scales = work.tile([P, GROUPS[gi]], U8, name="h_scales", tag="h_scales", bufs=4, align_bytes=64)
+            codes = work.tile([P, GROUPS[gi]], U32, name="h_codes", tag="h_codes", bufs=6, align_bytes=64)
+            scales = work.tile([P, GROUPS[gi]], U8, name="h_scales", tag="h_scales", bufs=6, align_bytes=64)
             quantize(codes[:], scales[:], h_grouped[(gi, b)][:])
             h_q[(gi, b)] = (codes, scales)
 
@@ -253,70 +319,129 @@ def tile_list_codebook_phoneme_logits_kernel(
             rows = out[step * per_bank * P : (step + 1) * per_bank * P, j0 : j0 + n]
             nc.sync.dma_start(rows.rearrange("(i p) j -> p i j", p=P), logits[:])
 
-        def permute_w3():
+        def permute_w3_words():
             nc.vector.tensor_copy(
                 w3_w[:].rearrange("p (b t m) -> p b t m", b=HALVES, t=PACK),
                 w3_w_raw[:].rearrange("p (b m t) -> p b t m", b=HALVES, t=PACK),
             )
+
+        def permute_w3_scales():
             nc.vector.tensor_copy(
                 w3_s[:].rearrange("p (b t m) -> p b t m", b=HALVES, t=PACK),
                 w3_s_raw[:].rearrange("p (b m t) -> p b t m", b=HALVES, t=PACK),
             )
 
-        gather_scales("cur", cur_list, 0)
         gather_scales("left", left_list, 0)
-        cast_weight("w1_0", w1_raw[0], "s")
-        quantize(w1_q[0][:], w1_s[0][:], grouped["w1_0"][:])
-        gather_words("cur", cur_list, 0)
+        gather_scales("left", left_list, 1)
+        gather_scales("left", left_list, 2)
         gather_words("left", left_list, 0)
-        for jt in range(2):
-            square("cur", 0, 0, jt)
-        for jt in range(2):
-            square("left", 0, 0, jt)
-        gather("cur", 1)
-        gather("left", 1)
-        gather("right", 0)
+        gather_words("left", left_list, 1)
+        gather_words("left", left_list, 2)
+        cast_weight("w1_0", w1_raw[0], "v")
+        quantize(w1_q[0][:], w1_s[0][:], grouped["w1_0"][:])
+        gather_scales("cur", cur_list, 0)
+        gather_words("cur", cur_list, 0)
+        gather_scales("cur", cur_list, 1)
+        gather_words("cur", cur_list, 1)
         cast_weight("w1_1", w1_raw[1], "v")
-        permute_w3()
         quantize(w1_q[1][:], w1_s[1][:], grouped["w1_1"][:])
-        squares_of(1, 0, (0, 1))
-        hidden_pair(0, 0, 0)
-        squares_of(1, 0, (2, 3))
-        gather("right", 1)
+        gather_scales("cur", cur_list, 2)
+        gather_words("cur", cur_list, 2)
+        gather_scales("right", right_list, 0)
+        gather_words("right", right_list, 0)
+        permute_w3_words()
+        permute_w3_scales()
+        square("left", 0, 0, 0)
+        square("left", 0, 0, 1)
+        square("left", 1, 0, 0)
+        square("left", 1, 0, 1)
+        square("left", 1, 0, 2)
+        square("left", 1, 0, 3)
+        square("left", 2, 0, 0)
+        square("left", 2, 0, 1)
+        square("left", 0, 1, 0)
+        square("left", 0, 1, 1)
+        square("cur", 0, 0, 0)
+        square("cur", 0, 0, 1)
+        energy_log(0, 0, 0)
+        energy_log(0, 0, 1)
+        square("cur", 1, 0, 0)
+        square("cur", 1, 0, 1)
+        square("cur", 1, 0, 2)
+        square("cur", 1, 0, 3)
+        energy_log(1, 0, 0)
+        energy_log(1, 0, 1)
+        square("cur", 2, 0, 0)
+        square("cur", 2, 0, 1)
+        square("left", 1, 1, 0)
+        square("left", 1, 1, 1)
+        square("left", 1, 1, 2)
+        square("left", 1, 1, 3)
+        energy_log(1, 0, 2)
+        energy_log(1, 0, 3)
+        finish(0, 0, 0, "c")
+        finish(0, 0, 1, "c")
+        gather_scales("right", right_list, 1)
+        gather_words("right", right_list, 1)
         group_hidden(0, 0, "v")
-        hidden_pair(1, 0, 0)
+        square("cur", 1, 1, 0)
+        square("cur", 1, 1, 1)
+        square("cur", 1, 1, 2)
+        square("cur", 1, 1, 3)
+        energy_log(2, 0, 0)
+        energy_log(2, 0, 1)
+        finish(1, 0, 0, "c")
+        finish(1, 0, 1, "c")
         quantize_hidden(0, 0)
-        squares_of(0, 1, (0, 1))
-        gather("cur", 2)
-        hidden_pair(1, 0, 2)
-        squares_of(1, 1, (0, 1))
-        cast_weight("w4_0", w4_raw[0], "s")
-        gather("left", 2)
+        finish(1, 0, 2, "c")
+        finish(1, 0, 3, "c")
+        gather_scales("right", right_list, 2)
+        gather_words("right", right_list, 2)
         group_hidden(1, 0, "v")
-        hidden_pair(0, 1, 0)
-        squares_of(1, 1, (2, 3))
+        square("cur", 0, 1, 0)
+        square("cur", 0, 1, 1)
+        energy_log(1, 1, 0)
+        energy_log(1, 1, 1)
+        cast_weight("w4_0", w4_raw[0], "s", 0, 2)
+        cast_weight("w4_0", w4_raw[0], "s", 1, 2)
+        finish(2, 0, 0, "c")
+        finish(2, 0, 1, "c")
         quantize_hidden(1, 0)
-        quantize(w4_q[0][:], w4_s[0][:], grouped["w4_0"][:])
-        cast_weight("w4_1", w4_raw[1], "v")
-        group_hidden(0, 1, "v")
-        gather("right", 2)
-        hidden_pair(1, 1, 0)
-        squares_of(2, 0, (0, 1))
-        quantize_hidden(0, 1)
-        quantize(w4_q[1][:], w4_s[1][:], grouped["w4_1"][:])
-        hidden_pair(1, 1, 2)
-        squares_of(2, 1, (0, 1))
-        group_hidden(1, 1, "v")
-        hidden_pair(2, 0, 0)
-        classify(0, 0, "ss"[0])
-        classify(0, 1, "ss"[1])
-        quantize_hidden(1, 1)
         group_hidden(2, 0, "v")
-        hidden_pair(2, 1, 0)
+        square("left", 2, 1, 0)
+        square("left", 2, 1, 1)
+        square("cur", 2, 1, 0)
+        square("cur", 2, 1, 1)
+        energy_log(1, 1, 2)
+        energy_log(1, 1, 3)
+        cast_weight("w4_1", w4_raw[1], "s", 0, 2)
+        cast_weight("w4_1", w4_raw[1], "s", 1, 2)
+        quantize(w4_q[0][:], w4_s[0][:], grouped["w4_0"][:])
+        finish(1, 1, 0, "c")
+        finish(1, 1, 1, "c")
+        finish(1, 1, 2, "c")
+        finish(1, 1, 3, "c")
         quantize_hidden(2, 0)
+        group_hidden(1, 1, "v")
+        quantize(w4_q[1][:], w4_s[1][:], grouped["w4_1"][:])
+        energy_log(0, 1, 0)
+        energy_log(0, 1, 1)
+        finish(0, 1, 0, "c")
+        finish(0, 1, 1, "c")
+        quantize_hidden(1, 1)
+        group_hidden(0, 1, "v")
+        energy_log(2, 1, 0)
+        energy_log(2, 1, 1)
+        classify(1, 0, "s", "ab")
+        classify(1, 1, "s", "ab")
+        classify(1, 2, "s", "ab")
+        classify(1, 3, "s", "ab")
+        finish(2, 1, 0, "c")
+        finish(2, 1, 1, "c")
+        quantize_hidden(0, 1)
         group_hidden(2, 1, "v")
+        classify(0, 0, "s", "c")
+        classify(0, 1, "s", "c")
         quantize_hidden(2, 1)
-        for step in range(4):
-            classify(1, step, "ssss"[step])
-        classify(2, 0, "v", "c")
-        classify(2, 1, "s", "c")
+        classify(2, 0, "v", "energy")
+        classify(2, 1, "s", "energy")

@@ -68,7 +68,7 @@ def tile_list_codebook_phoneme_logits_kernel(
             elif engine == "s":
                 nc.scalar.activation(o, i_, ACT.Copy)
             else:
-                nc.gpsimd.tensor_scalar(o, i_, 1.0, 0.0, ALU.mult, ALU.add)
+                nc.gpsimd.tensor_scalar(dst, src.rearrange("p t c -> p c t"), 1.0, 0.0, ALU.mult, ALU.add)
 
         def quantize(codes, scales, grouped):
             nc.vector.quantize_mx(codes.bitcast(FP8X4), scales, grouped.rearrange("p c t -> p (c t)"))
@@ -331,117 +331,117 @@ def tile_list_codebook_phoneme_logits_kernel(
                 w3_s_raw[:].rearrange("p (b m t) -> p b t m", b=HALVES, t=PACK),
             )
 
-        gather_scales("left", left_list, 0)
-        gather_scales("left", left_list, 1)
-        gather_scales("left", left_list, 2)
         gather_words("left", left_list, 0)
         gather_words("left", left_list, 1)
         gather_words("left", left_list, 2)
         cast_weight("w1_0", w1_raw[0], "v")
         quantize(w1_q[0][:], w1_s[0][:], grouped["w1_0"][:])
+        permute_w3_words()
+        permute_w3_scales()
+        gather_scales("left", left_list, 0)
+        gather_scales("left", left_list, 1)
+        gather_scales("left", left_list, 2)
+        square("left", 0, 1, 0)
+        square("left", 0, 1, 1)
         gather_scales("cur", cur_list, 0)
         gather_words("cur", cur_list, 0)
+        square("left", 1, 0, 0)
+        square("left", 1, 0, 1)
+        cast_weight("w4_0", w4_raw[0], "g", 1, 2)
+        square("left", 0, 0, 0)
+        square("left", 0, 0, 1)
         gather_scales("cur", cur_list, 1)
         gather_words("cur", cur_list, 1)
-        cast_weight("w1_1", w1_raw[1], "v")
+        square("left", 2, 0, 0)
+        square("left", 2, 0, 1)
+        square("left", 1, 0, 2)
+        square("left", 1, 0, 3)
+        square("cur", 0, 0, 0)
+        square("cur", 0, 0, 1)
+        square("left", 1, 1, 0)
+        square("left", 1, 1, 1)
+        square("cur", 1, 0, 2)
+        square("cur", 1, 0, 3)
+        cast_weight("w1_1", w1_raw[1], "g")
+        energy_log(0, 0, 0)
+        energy_log(0, 0, 1)
+        cast_weight("w4_0", w4_raw[0], "g", 0, 2)
         quantize(w1_q[1][:], w1_s[1][:], grouped["w1_1"][:])
         gather_scales("cur", cur_list, 2)
         gather_words("cur", cur_list, 2)
-        gather_scales("right", right_list, 0)
-        gather_words("right", right_list, 0)
-        permute_w3_words()
-        permute_w3_scales()
-        square("left", 0, 0, 0)
-        square("left", 0, 0, 1)
-        square("left", 1, 0, 0)
-        square("left", 1, 0, 1)
-        square("left", 1, 0, 2)
-        square("left", 1, 0, 3)
-        square("left", 2, 0, 0)
-        square("left", 2, 0, 1)
-        square("left", 0, 1, 0)
-        square("left", 0, 1, 1)
-        square("cur", 0, 0, 0)
-        square("cur", 0, 0, 1)
-        energy_log(0, 0, 0)
-        energy_log(0, 0, 1)
         square("cur", 1, 0, 0)
         square("cur", 1, 0, 1)
-        square("cur", 1, 0, 2)
-        square("cur", 1, 0, 3)
-        energy_log(1, 0, 0)
-        energy_log(1, 0, 1)
         square("cur", 2, 0, 0)
         square("cur", 2, 0, 1)
-        square("left", 1, 1, 0)
-        square("left", 1, 1, 1)
-        square("left", 1, 1, 2)
-        square("left", 1, 1, 3)
         energy_log(1, 0, 2)
         energy_log(1, 0, 3)
-        finish(0, 0, 0, "c")
-        finish(0, 0, 1, "c")
+        square("left", 1, 1, 2)
+        square("left", 1, 1, 3)
         gather_scales("right", right_list, 1)
         gather_words("right", right_list, 1)
-        group_hidden(0, 0, "v")
-        square("cur", 1, 1, 0)
-        square("cur", 1, 1, 1)
+        energy_log(1, 0, 0)
+        energy_log(1, 0, 1)
         square("cur", 1, 1, 2)
         square("cur", 1, 1, 3)
+        square("cur", 1, 1, 0)
+        square("cur", 1, 1, 1)
+        gather_scales("right", right_list, 0)
+        gather_words("right", right_list, 0)
+        finish(0, 0, 0, "c")
+        finish(0, 0, 1, "c")
         energy_log(2, 0, 0)
         energy_log(2, 0, 1)
-        finish(1, 0, 0, "c")
-        finish(1, 0, 1, "c")
-        quantize_hidden(0, 0)
-        finish(1, 0, 2, "c")
-        finish(1, 0, 3, "c")
-        gather_scales("right", right_list, 2)
-        gather_words("right", right_list, 2)
+        finish(1, 0, 0, "ab")
+        finish(1, 0, 1, "ab")
+        finish(1, 0, 2, "ab")
+        finish(1, 0, 3, "ab")
+        group_hidden(0, 0, "v")
+        quantize(w4_q[0][:], w4_s[0][:], grouped["w4_0"][:])
+        cast_weight("w4_1", w4_raw[1], "g", 1, 2)
+        cast_weight("w4_1", w4_raw[1], "g", 0, 2)
+        quantize(w4_q[1][:], w4_s[1][:], grouped["w4_1"][:])
         group_hidden(1, 0, "v")
-        square("cur", 0, 1, 0)
-        square("cur", 0, 1, 1)
-        energy_log(1, 1, 0)
-        energy_log(1, 1, 1)
-        cast_weight("w4_0", w4_raw[0], "s", 0, 2)
-        cast_weight("w4_0", w4_raw[0], "s", 1, 2)
-        finish(2, 0, 0, "c")
-        finish(2, 0, 1, "c")
-        quantize_hidden(1, 0)
-        group_hidden(2, 0, "v")
-        square("left", 2, 1, 0)
-        square("left", 2, 1, 1)
-        square("cur", 2, 1, 0)
-        square("cur", 2, 1, 1)
         energy_log(1, 1, 2)
         energy_log(1, 1, 3)
-        cast_weight("w4_1", w4_raw[1], "s", 0, 2)
-        cast_weight("w4_1", w4_raw[1], "s", 1, 2)
-        quantize(w4_q[0][:], w4_s[0][:], grouped["w4_0"][:])
-        finish(1, 1, 0, "c")
-        finish(1, 1, 1, "c")
+        square("cur", 0, 1, 0)
+        square("cur", 0, 1, 1)
+        gather_scales("right", right_list, 2)
+        gather_words("right", right_list, 2)
+        energy_log(1, 1, 0)
+        energy_log(1, 1, 1)
+        finish(2, 0, 0, "c")
+        finish(2, 0, 1, "c")
+        square("cur", 2, 1, 0)
+        square("cur", 2, 1, 1)
+        quantize_hidden(1, 0)
+        finish(1, 1, 0, "energy")
+        finish(1, 1, 1, "energy")
         finish(1, 1, 2, "c")
         finish(1, 1, 3, "c")
-        quantize_hidden(2, 0)
         group_hidden(1, 1, "v")
-        quantize(w4_q[1][:], w4_s[1][:], grouped["w4_1"][:])
+        quantize_hidden(1, 1)
+        group_hidden(2, 0, "s")
         energy_log(0, 1, 0)
         energy_log(0, 1, 1)
-        finish(0, 1, 0, "c")
-        finish(0, 1, 1, "c")
-        quantize_hidden(1, 1)
+        square("left", 2, 1, 0)
+        square("left", 2, 1, 1)
+        quantize_hidden(0, 0)
+        finish(0, 1, 0, "ab")
+        finish(0, 1, 1, "ab")
         group_hidden(0, 1, "v")
         energy_log(2, 1, 0)
         energy_log(2, 1, 1)
-        classify(1, 0, "s", "ab")
-        classify(1, 1, "s", "ab")
-        classify(1, 2, "s", "ab")
-        classify(1, 3, "s", "ab")
         finish(2, 1, 0, "c")
         finish(2, 1, 1, "c")
+        classify(1, 3, "s", "ab")
+        classify(1, 1, "s", "ab")
+        classify(1, 0, "s", "ab")
         quantize_hidden(0, 1)
-        group_hidden(2, 1, "v")
-        classify(0, 0, "s", "c")
+        classify(0, 0, "s", "energy")
+        classify(1, 2, "s", "ab")
         classify(0, 1, "s", "c")
+        group_hidden(2, 1, "v")
         quantize_hidden(2, 1)
-        classify(2, 0, "v", "energy")
-        classify(2, 1, "s", "energy")
+        quantize_hidden(2, 0)
+        classify(2, 0, "s", "c")
+        classify(2, 1, "v", "ab")

from contextlib import ExitStack

import concourse.mybir as mybir
from concourse.masks import make_identity

K, H, N, T, S = 512, 1024, 512, 2048, 1024
FLOPS = 2 * K * H * S * 3 + 2 * H * N * S

F32 = mybir.dt.float32
BF16 = mybir.dt.bfloat16
I32 = mybir.dt.int32
U32 = mybir.dt.uint32
U16 = mybir.dt.uint16
U8 = mybir.dt.uint8
FP8X4 = mybir.dt.float8_e4m3fn_x4
FP4X4 = mybir.dt.float4_e2m1fn_x4
ACT = mybir.ActivationFunctionType
ALU = mybir.AluOpType

P = 128
PACK = 4
PASS = P * PACK
BANK = 512
HALVES = H // PASS
GROUPS = [256, 512, 256]


def tile_list_codebook_phoneme_logits_kernel(
    tc, tab_words, tab_scales, offs, offs2, offs3, w1, w2_words, w2_scales, w3_words, w3_scales, g, w4, out
):
    nc = tc.nc
    with ExitStack() as ctx:
        keep = ctx.enter_context(tc.tile_pool(name="keep", bufs=1))
        work = ctx.enter_context(tc.tile_pool(name="work", bufs=1))
        psum = ctx.enter_context(tc.psum_pool(name="psum", bufs=1))

        cur_list = keep.tile([P, S // 16], U16, name="cur_list")
        left_list = keep.tile([P, S // 16], U16, name="left_list")
        right_list = keep.tile([P, S // 16], U16, name="right_list")
        tab_w = keep.tile([P, T], I32, name="tab_w", align_bytes=64)
        tab_s = keep.tile([P, T], U8, name="tab_s", align_bytes=64)
        w2_w = keep.tile([P, 2 * H], U8, name="w2_w", align_bytes=64)
        w2_s = keep.tile([P, H], U8, name="w2_s", align_bytes=64)
        w3_w_raw = keep.tile([P, H], I32, name="w3_w_raw", align_bytes=64)
        w3_s_raw = keep.tile([P, H], U8, name="w3_s_raw", align_bytes=64)
        w3_w = keep.tile([P, H], I32, name="w3_w", align_bytes=64)
        w3_s = keep.tile([P, H], U8, name="w3_s", align_bytes=64)
        gain = keep.tile([P, HALVES, PACK], F32, name="gain")
        ident = keep.tile([P, P], F32, name="ident", align_bytes=64)
        one = keep.tile([P, 1], F32, name="one")
        warm = keep.tile([P, 1], F32, name="warm")
        w1_raw = [keep.tile([P, PACK, PASS], F32, name=f"w1_raw{b}", align_bytes=64) for b in range(HALVES)]
        w4_raw = [keep.tile([P, PACK, N], F32, name=f"w4_raw{b}", align_bytes=64) for b in range(HALVES)]
        w1_q = [keep.tile([P, PASS], U32, name=f"w1_q{b}", align_bytes=64) for b in range(HALVES)]
        w1_s = [keep.tile([P, PASS], U8, name=f"w1_s{b}", align_bytes=64) for b in range(HALVES)]
        w4_q = [keep.tile([P, N], U32, name=f"w4_q{b}", align_bytes=64) for b in range(HALVES)]
        w4_s = [keep.tile([P, N], U8, name=f"w4_s{b}", align_bytes=64) for b in range(HALVES)]

        def load_scales(queue, plane, rows):
            for q in range(4):
                queue.dma_start(plane[32 * q : 32 * q + 4, :].bitcast(I32), rows[0, 4 * q : 4 * q + 4, :].bitcast(I32))

        def interleave(engine, dst, src):
            o = dst.rearrange("p (c i) t -> p c t i", i=4)
            i_ = src.rearrange("p t (c i) -> p c t i", i=4)
            if engine == "v":
                nc.vector.tensor_copy(o, i_)
            elif engine == "s":
                nc.scalar.activation(o, i_, ACT.Copy)
            else:
                nc.gpsimd.tensor_scalar(dst, src.rearrange("p t c -> p c t"), 1.0, 0.0, ALU.mult, ALU.add)

        def quantize(codes, scales, grouped):
            nc.vector.quantize_mx(codes.bitcast(FP8X4), scales, grouped.rearrange("p c t -> p (c t)"))

        nc.gpsimd.memset(tab_s[:].bitcast(I32), 0)
        nc.vector.memset(one[:], 1.0)
        nc.vector.memset(w2_s[:].bitcast(I32), 0)
        nc.vector.memset(w3_s_raw[:].bitcast(I32), 0)
        nc.scalar.activation(warm[:], one[:], ACT.Ln)
        make_identity(nc, ident[:])
        w1_rows = w1.rearrange("(p j) c -> p j c", j=PACK)
        w4_rows = w4.rearrange("(b p j) n -> b p j n", b=HALVES, j=PACK)
        nc.sync.dma_start(left_list[:], offs2)
        nc.sync.dma_start(w2_w[:].bitcast(I32), w2_words[0].bitcast(I32))
        load_scales(nc.sync, tab_s, tab_scales)
        nc.sync.dma_start(tab_w[:], tab_words[0].rearrange("p t i -> p (t i)").bitcast(I32))
        load_scales(nc.sync, w2_s, w2_scales)
        nc.sync.dma_start(w1_raw[0][:], w1_rows[:, :, 0:PASS])
        nc.sync.dma_start(cur_list[:], offs)
        nc.sync.dma_start(w1_raw[1][:], w1_rows[:, :, PASS:H])
        nc.sync.dma_start(right_list[:], offs3)
        nc.sync.dma_start(w3_w_raw[:], w3_words[0].rearrange("p e i -> p (e i)").bitcast(I32))
        nc.sync.dma_start(w4_raw[0][:], w4_rows[0])
        nc.sync.dma_start(w4_raw[1][:], w4_rows[1])
        load_scales(nc.sync, w3_s_raw, w3_scales)
        nc.sync.dma_start(gain[:], g.rearrange("(b p t) -> p b t", b=HALVES, t=PACK))

        banks = [psum.tile([P, BANK], F32, name=f"bank{i}") for i in range(8)]
        rings = {"ab": banks[0:4], "energy": banks[4:6], "c": banks[6:8]}
        turns = {name: 0 for name in rings}

        def next_bank(name):
            ring = rings[name]
            turns[name] += 1
            return ring[(turns[name] - 1) % len(ring)]

        starts = [sum(GROUPS[:i]) for i in range(len(GROUPS))]
        picked = {}

        def gather_scales(name, lst, gi):
            n, j0 = GROUPS[gi], starts[gi]
            tile = keep.tile([P, n], U8, name=f"{name}_s{gi}", align_bytes=64)
            nc.vector.tensor_copy(tile[:], tab_s[:].indirect(lst[:, j0 // 16 : (j0 + n) // 16]))
            picked[(name, "s", gi)] = tile

        def gather_words(name, lst, gi):
            n, j0 = GROUPS[gi], starts[gi]
            tile = keep.tile([P, n], U32, name=f"{name}_w{gi}", align_bytes=64)
            nc.vector.tensor_copy(tile[:], tab_w[:].bitcast(U32).indirect(lst[:, j0 // 16 : (j0 + n) // 16]))
            picked[(name, "w", gi)] = tile

        lists = {"left": left_list, "cur": cur_list, "right": right_list}

        def gather(name, gi):
            gather_scales(name, lists[name], gi)
            gather_words(name, lists[name], gi)

        grouped = {}

        def cast_weight(name, raw, engine, part=0, parts=1):
            if name not in grouped:
                grouped[name] = keep.tile([P, PASS, PACK], BF16, name=f"{name}_bf", align_bytes=64)
            cols = slice(part * PASS // parts, (part + 1) * PASS // parts)
            interleave(engine, grouped[name][:, cols, :], raw[:, :, cols])

        squares = {}

        def square(which, gi, b, jt):
            bank = next_bank("ab")
            cols = slice(jt * P, (jt + 1) * P)
            if which == "cur":
                rhs, rhs_scale = w1_q[b][:].bitcast(FP8X4), w1_s[b][:]
            else:
                rhs = w2_w[:, 2 * b * PASS : 2 * (b + 1) * PASS].bitcast(FP4X4)
                rhs_scale = w2_s[:, b * PASS : (b + 1) * PASS]
            nc.tensor.matmul_mx(
                bank[:],
                lhsT=picked[(which, "w", gi)][:, cols].bitcast(FP8X4),
                lhsT_scale=picked[(which, "s", gi)][:, cols],
                rhs=rhs,
                rhs_scale=rhs_scale,
                start=True,
                stop=True,
            )
            sq = work.tile([P, PACK, P], F32, name="sq", tag="sq", bufs=26, align_bytes=64)
            nc.scalar.activation(sq[:], bank[:].rearrange("p (m t) -> p t m", t=PACK), ACT.Square)
            squares[(which, gi, b, jt)] = sq

        w2p_w = [keep.tile([P, 2 * PASS], U8, name=f"w2p_w{b}", align_bytes=64) for b in range(HALVES)]
        w2p_s = [keep.tile([P, PASS], U8, name=f"w2p_s{b}", align_bytes=64) for b in range(HALVES)]

        def permute_w2(b):
            nc.vector.tensor_copy(
                w2p_w[b][:].rearrange("p (t m e) -> p t m e", t=PACK, e=2),
                w2_w[:, 2 * b * PASS : 2 * (b + 1) * PASS].rearrange("p (m t e) -> p t m e", t=PACK, e=2),
            )
            nc.vector.tensor_copy(
                w2p_s[b][:].rearrange("p (t m) -> p t m", t=PACK),
                w2_s[:, b * PASS : (b + 1) * PASS].rearrange("p (m t) -> p t m", t=PACK),
            )

        def cast_permuted(name, raw, engine):
            tile = keep.tile([P, PASS, PACK], BF16, name=f"{name}_bf", align_bytes=64)
            o = tile[:].rearrange("p (t m) j -> p m j t", t=PACK)
            i_ = raw[:].rearrange("p j (m t) -> p m j t", t=PACK)
            if engine == "v":
                nc.vector.tensor_copy(o, i_)
            elif engine == "s":
                nc.scalar.activation(o, i_, ACT.Copy)
            else:
                nc.gpsimd.tensor_scalar(o, i_, 1.0, 0.0, ALU.mult, ALU.add)
            grouped[name] = tile

        direct = {}

        def square_direct(which, gi, b, step):
            n = GROUPS[gi]
            per_bank = BANK // n
            bank = next_bank("ab")[:]
            for i in range(per_bank):
                t = step * per_bank + i
                if which == "cur":
                    lhsT, lhsT_scale = w1_q[b][:, t * P : (t + 1) * P].bitcast(FP8X4), w1_s[b][:, t * P : (t + 1) * P]
                else:
                    lhsT, lhsT_scale = w2p_w[b][:, 2 * t * P : 2 * (t + 1) * P].bitcast(FP4X4), w2p_s[b][:, t * P : (t + 1) * P]
                nc.tensor.matmul_mx(
                    bank[:, i * n : (i + 1) * n],
                    lhsT=lhsT,
                    lhsT_scale=lhsT_scale,
                    rhs=picked[(which, "w", gi)][:].bitcast(FP8X4),
                    rhs_scale=picked[(which, "s", gi)][:],
                    start=True,
                    stop=True,
                )
            sq = work.tile([P, BANK], F32, name="sqd", tag="sqd", bufs=8, align_bytes=64)
            nc.scalar.activation(sq[:], bank, ACT.Square)
            direct[(which, gi, b, step)] = sq

        summed = {}

        def add_direct(gi, b, step, engine):
            total = work.tile([P, BANK], F32, name="total", tag="total", bufs=4, align_bytes=64)
            eng = nc.vector if engine == "v" else nc.gpsimd
            eng.tensor_tensor(total[:], direct[("cur", gi, b, step)][:], direct[("left", gi, b, step)][:], ALU.add)
            summed[(gi, b, step)] = total

        def log_direct(gi, b, step):
            n = GROUPS[gi]
            logs = work.tile([P, BANK // n, n], F32, name="logs", tag="logs", bufs=10, align_bytes=64)
            nc.scalar.activation(logs[:].rearrange("p i n -> p (i n)"), summed[(gi, b, step)][:], ACT.Ln, bias=one[:])
            logged[(gi, b, step)] = logs

        planes = {}

        logged = {}

        def energy_log(gi, b, step):
            n = GROUPS[gi]
            per_bank = BANK // n
            ts = range(step * per_bank, (step + 1) * per_bank)
            energy = next_bank("energy")[:].rearrange("p (i n) -> p i n", n=n)
            for i, t in enumerate(ts):
                for jt in reversed(range(n // P)):
                    for which in ("cur", "left"):
                        nc.tensor.matmul(
                            energy[:, i, jt * P : (jt + 1) * P],
                            lhsT=squares[(which, gi, b, jt)][:, t, :],
                            rhs=ident[:],
                            start=(which == "cur"),
                            stop=(which == "left"),
                            is_transpose=True,
                        )
            logs = work.tile([P, per_bank, n], F32, name="logs", tag="logs", bufs=10, align_bytes=64)
            nc.scalar.activation(logs[:], energy, ACT.Ln, bias=one[:])
            logged[(gi, b, step)] = logs

        def finish(gi, b, step, ring="c"):
            n = GROUPS[gi]
            per_bank = BANK // n
            ts = range(step * per_bank, (step + 1) * per_bank)
            logs = logged[(gi, b, step)]
            c_bank = next_bank(ring)[:].rearrange("p (i n) -> p i n", n=n)
            for i, t in enumerate(ts):
                cols = slice(b * PASS + t * P, b * PASS + (t + 1) * P)
                nc.tensor.matmul_mx(
                    c_bank[:, i, :],
                    lhsT=w3_w[:, cols].bitcast(FP8X4),
                    lhsT_scale=w3_s[:, cols],
                    rhs=picked[("right", "w", gi)][:].bitcast(FP8X4),
                    rhs_scale=picked[("right", "s", gi)][:],
                    start=True,
                    stop=True,
                )
            if step == 0:
                planes[(gi, b)] = work.tile([P, PACK, n], BF16, name="h_planes", tag="h_planes", bufs=3, align_bytes=64)
            for i, t in enumerate(ts):
                nc.vector.scalar_tensor_tensor(
                    planes[(gi, b)][:, t, :], logs[:, i, :], gain[:, b, t : t + 1], c_bank[:, i, :], ALU.mult, ALU.add
                )

        def hidden_pair(gi, b, step):
            energy_log(gi, b, step)
            energy_log(gi, b, step + 1)
            finish(gi, b, step)
            finish(gi, b, step + 1)

        def squares_of(gi, b, jts):
            for jt in jts:
                square("left", gi, b, jt)
                square("cur", gi, b, jt)

        h_grouped = {}
        h_q = {}

        def group_hidden(gi, b, engine):
            tile = work.tile([P, GROUPS[gi], PACK], BF16, name="h_grouped", tag="h_grouped", bufs=3, align_bytes=64)
            interleave(engine, tile[:], planes[(gi, b)][:])
            h_grouped[(gi, b)] = tile

        def quantize_hidden(gi, b):
            codes = work.tile([P, GROUPS[gi]], U32, name="h_codes", tag="h_codes", bufs=6, align_bytes=64)
            scales = work.tile([P, GROUPS[gi]], U8, name="h_scales", tag="h_scales", bufs=6, align_bytes=64)
            quantize(codes[:], scales[:], h_grouped[(gi, b)][:])
            h_q[(gi, b)] = (codes, scales)

        def classify(gi, step, engine, ring="ab"):
            n, j0 = GROUPS[gi], starts[gi]
            per_bank = BANK // n
            bank = next_bank(ring)[:].rearrange("p (i n) -> p i n", n=n)
            for i in range(per_bank):
                cols = slice((step * per_bank + i) * P, (step * per_bank + i + 1) * P)
                for b in range(HALVES):
                    codes, scales = h_q[(gi, b)]
                    nc.tensor.matmul_mx(
                        bank[:, i, :],
                        lhsT=w4_q[b][:, cols].bitcast(FP8X4),
                        lhsT_scale=w4_s[b][:, cols],
                        rhs=codes[:].bitcast(FP8X4),
                        rhs_scale=scales[:],
                        start=(b == 0),
                        stop=(b == HALVES - 1),
                    )
            logits = work.tile([P, per_bank, n], F32, name="logits", tag="logits", bufs=4, align_bytes=64)
            if engine == "v":
                nc.vector.tensor_copy(logits[:], bank)
            else:
                nc.scalar.copy(logits[:], bank)
            rows = out[step * per_bank * P : (step + 1) * per_bank * P, j0 : j0 + n]
            nc.sync.dma_start(rows.rearrange("(i p) j -> p i j", p=P), logits[:])

        def permute_w3_words():
            nc.vector.tensor_copy(
                w3_w[:].rearrange("p (b t m) -> p b t m", b=HALVES, t=PACK),
                w3_w_raw[:].rearrange("p (b m t) -> p b t m", b=HALVES, t=PACK),
            )

        def permute_w3_scales():
            nc.vector.tensor_copy(
                w3_s[:].rearrange("p (b t m) -> p b t m", b=HALVES, t=PACK),
                w3_s_raw[:].rearrange("p (b m t) -> p b t m", b=HALVES, t=PACK),
            )

        gather_words("left", left_list, 0)
        gather_words("left", left_list, 1)
        gather_words("left", left_list, 2)
        cast_weight("w1_0", w1_raw[0], "v")
        quantize(w1_q[0][:], w1_s[0][:], grouped["w1_0"][:])
        permute_w3_words()
        permute_w3_scales()
        gather_scales("left", left_list, 0)
        gather_scales("left", left_list, 1)
        gather_scales("left", left_list, 2)
        square("left", 0, 1, 0)
        square("left", 0, 1, 1)
        gather_scales("cur", cur_list, 0)
        gather_words("cur", cur_list, 0)
        square("left", 1, 0, 0)
        square("left", 1, 0, 1)
        cast_weight("w4_0", w4_raw[0], "g", 1, 2)
        square("left", 0, 0, 0)
        square("left", 0, 0, 1)
        gather_scales("cur", cur_list, 1)
        gather_words("cur", cur_list, 1)
        square("left", 2, 0, 0)
        square("left", 2, 0, 1)
        square("left", 1, 0, 2)
        square("left", 1, 0, 3)
        square("cur", 0, 0, 0)
        square("cur", 0, 0, 1)
        square("left", 1, 1, 0)
        square("left", 1, 1, 1)
        square("cur", 1, 0, 2)
        square("cur", 1, 0, 3)
        cast_weight("w1_1", w1_raw[1], "g")
        energy_log(0, 0, 0)
        energy_log(0, 0, 1)
        cast_weight("w4_0", w4_raw[0], "g", 0, 2)
        quantize(w1_q[1][:], w1_s[1][:], grouped["w1_1"][:])
        gather_scales("cur", cur_list, 2)
        gather_words("cur", cur_list, 2)
        square("cur", 1, 0, 0)
        square("cur", 1, 0, 1)
        square("cur", 2, 0, 0)
        square("cur", 2, 0, 1)
        energy_log(1, 0, 2)
        energy_log(1, 0, 3)
        square("left", 1, 1, 2)
        square("left", 1, 1, 3)
        gather_scales("right", right_list, 1)
        gather_words("right", right_list, 1)
        energy_log(1, 0, 0)
        energy_log(1, 0, 1)
        square("cur", 1, 1, 2)
        square("cur", 1, 1, 3)
        square("cur", 1, 1, 0)
        square("cur", 1, 1, 1)
        gather_scales("right", right_list, 0)
        gather_words("right", right_list, 0)
        finish(0, 0, 0, "c")
        finish(0, 0, 1, "c")
        energy_log(2, 0, 0)
        energy_log(2, 0, 1)
        finish(1, 0, 0, "ab")
        finish(1, 0, 1, "ab")
        finish(1, 0, 2, "ab")
        finish(1, 0, 3, "ab")
        group_hidden(0, 0, "v")
        quantize(w4_q[0][:], w4_s[0][:], grouped["w4_0"][:])
        cast_weight("w4_1", w4_raw[1], "g", 1, 2)
        cast_weight("w4_1", w4_raw[1], "g", 0, 2)
        quantize(w4_q[1][:], w4_s[1][:], grouped["w4_1"][:])
        group_hidden(1, 0, "v")
        energy_log(1, 1, 2)
        energy_log(1, 1, 3)
        square("cur", 0, 1, 0)
        square("cur", 0, 1, 1)
        gather_scales("right", right_list, 2)
        gather_words("right", right_list, 2)
        energy_log(1, 1, 0)
        energy_log(1, 1, 1)
        finish(2, 0, 0, "c")
        finish(2, 0, 1, "c")
        square("cur", 2, 1, 0)
        square("cur", 2, 1, 1)
        quantize_hidden(1, 0)
        finish(1, 1, 0, "energy")
        finish(1, 1, 1, "energy")
        finish(1, 1, 2, "c")
        finish(1, 1, 3, "c")
        group_hidden(1, 1, "v")
        quantize_hidden(1, 1)
        group_hidden(2, 0, "s")
        energy_log(0, 1, 0)
        energy_log(0, 1, 1)
        square("left", 2, 1, 0)
        square("left", 2, 1, 1)
        quantize_hidden(0, 0)
        finish(0, 1, 0, "ab")
        finish(0, 1, 1, "ab")
        group_hidden(0, 1, "v")
        energy_log(2, 1, 0)
        energy_log(2, 1, 1)
        finish(2, 1, 0, "c")
        finish(2, 1, 1, "c")
        classify(1, 3, "s", "ab")
        classify(1, 1, "s", "ab")
        classify(1, 0, "s", "ab")
        quantize_hidden(0, 1)
        classify(0, 0, "s", "energy")
        classify(1, 2, "s", "ab")
        classify(0, 1, "s", "c")
        group_hidden(2, 1, "v")
        quantize_hidden(2, 1)
        quantize_hidden(2, 0)
        classify(2, 0, "s", "c")
        classify(2, 1, "v", "ab")
